import numpy as np
import ml_dtypes


def mxq(x, axis, fmt="e4m3"):
    dtype, down = {"e4m3": (ml_dtypes.float8_e4m3fn, 7), "e5m2": (ml_dtypes.float8_e5m2, 14)}[fmt]
    v = np.moveaxis(np.asarray(x, np.float32).astype(ml_dtypes.bfloat16).astype(np.float64), axis, -1)
    blocks = v.reshape(v.shape[:-1] + (-1, 32))
    amax = np.abs(blocks).max(-1, keepdims=True)
    byte = np.maximum(np.where(amax > 0, np.frexp(amax)[1] - 1 + 127, 0) - down, 1)
    scale = np.exp2(byte - 127.0)
    codes = (blocks / scale).astype(np.float32).astype(dtype).astype(np.float64)
    return np.moveaxis((codes * scale).reshape(v.shape), -1, axis)


WIDE = False


def mx_kscale(k):
    if not WIDE:
        return np.ones(k)
    levels = np.array([30, -30])
    if k % 512:
        return np.exp2(np.random.permutation(np.resize(levels, k // 32))).repeat(32)
    a = np.empty((k // 512, 16))
    for p in range(k // 512):
        a[p, :8] = np.random.permutation(np.resize(levels, 8))
        for g in range(8):
            far = levels[np.abs(levels - a[p, g]) >= 10]
            a[p, g + 8] = far[np.random.randint(len(far))]
    return np.exp2(a.ravel()).repeat(32)


def f64(x):
    return np.asarray(x).astype(np.float64)


def striped(idx):
    return np.tile(np.asarray(idx).reshape(-1, 16).T, (8, 1)).astype(np.uint16)


def unstriped(offs):
    return offs[:16].T.reshape(-1).astype(np.int64)


E2M1 = np.array([0.0, 0.5, 1.0, 1.5, 2.0, 3.0, 4.0, 6.0, -0.0, -0.5, -1.0, -1.5, -2.0, -3.0, -4.0, -6.0])


def pack_weight(w, fmt):
    k, n = w.shape
    w = f64(np.asarray(w, np.float32).astype(ml_dtypes.bfloat16)).reshape(k // 32, 32, n)
    amax = np.abs(w).max(1)
    if fmt in ("e4m3", "e5m2"):
        byte = np.frexp(amax)[1] - 1 + 127 - (7 if fmt == "e4m3" else 14)
    else:
        mant, ex = np.frexp(amax / 6.0)
        byte = np.where(mant > 0.5, ex, ex - 1) + 127
    byte = np.clip(np.where(amax > 0, byte, 1), 1, 254)
    scaled = (w * np.exp2(127.0 - byte)[:, None, :]).reshape(k, n).astype(np.float32)
    by_word = np.ascontiguousarray(scaled.reshape(k // 512, 128, 4, n).transpose(0, 1, 3, 2))
    if fmt in ("e4m3", "e5m2"):
        words = by_word.astype(ml_dtypes.float8_e4m3fn if fmt == "e4m3" else ml_dtypes.float8_e5m2).view(np.uint8)
    else:
        c = by_word.astype(ml_dtypes.float4_e2m1fn).view(np.uint8) & 0xF
        words = (c[..., 0::2] | (c[..., 1::2] << 4)).reshape(k // 512, 128, 2 * n)
    return np.ascontiguousarray(words), np.ascontiguousarray(byte.astype(np.uint8).reshape(k // 512, 16, n))


def unpack_weight(words, scales, fmt):
    g, _, n = scales.shape
    words = np.ascontiguousarray(words).reshape(g, 128, n, -1)
    if fmt in ("e4m3", "e5m2"):
        vals = words.view(ml_dtypes.float8_e4m3fn if fmt == "e4m3" else ml_dtypes.float8_e5m2).astype(np.float64)
    else:
        nib = np.empty((g, 128, n, 4), np.uint8)
        nib[..., 0::2] = words & 0xF
        nib[..., 1::2] = words >> 4
        vals = E2M1[nib]
    vals = vals * np.repeat(np.exp2(scales.astype(np.float64) - 127.0), 8, axis=1)[..., None]
    return vals.transpose(0, 1, 3, 2).reshape(g * 512, n)


K, T, J, R, C, O, N, L = 512, 2048, 256, 512, 512, 256, 256, 512


def setup_inputs():
    n = np.random.standard_normal
    idx = np.random.permutation(T)[:J]
    idx2 = np.random.permutation(T)[:J]
    idx3 = np.random.permutation(C)[:J]
    idx4 = np.random.permutation(C)[:J]
    idx5 = np.random.permutation(C)[:O]
    idx6 = np.random.permutation(C)[:O]
    fk = mx_kscale(K)
    fr = mx_kscale(R)
    fl = mx_kscale(L)
    xtp = pack_weight(n((K, T)) / fk[:, None], "e2m1")
    wp = pack_weight(n((K, R)) * 1 / np.sqrt(K) * fk[:, None] * fr, "e5m2")
    w2p = pack_weight(n((K, R)) * 1 / np.sqrt(K) * fk[:, None] * fr, "e4m3")
    wbp = pack_weight(n((R, N)) * 1 / np.sqrt(R) / fr[:, None], "e4m3")
    sxp = pack_weight(n((L, O)) / fl[:, None], "e5m2")
    wsp = pack_weight(n((L, N)) * 1 / np.sqrt(L) * fl[:, None], "e4m3")
    return {
        "xt_words": xtp[0],
        "xt_scales": xtp[1],
        "w_words": wp[0],
        "w_scales": wp[1],
        "w2_words": w2p[0],
        "w2_scales": w2p[1],
        "wb_words": wbp[0],
        "wb_scales": wbp[1],
        "sx_words": sxp[0],
        "sx_scales": sxp[1],
        "ws_words": wsp[0],
        "ws_scales": wsp[1],
        "offs": striped(idx),
        "offs2": striped(idx2),
        "offs3": striped(idx3),
        "offs4": striped(idx4),
        "offs5": striped(idx5),
        "offs6": striped(idx6),
    }


def reference(xt_words, xt_scales, w_words, w_scales, w2_words, w2_scales, wb_words, wb_scales, sx_words, sx_scales, ws_words, ws_scales, offs, offs2, offs3, offs4, offs5, offs6):
    idx = unstriped(offs)
    idx2 = unstriped(offs2)
    idx3 = unstriped(offs3)
    idx4 = unstriped(offs4)
    idx5 = unstriped(offs5)
    idx6 = unstriped(offs6)
    xtu = unpack_weight(xt_words, xt_scales, "e2m1")
    wu = unpack_weight(w_words, w_scales, "e5m2")
    w2u = unpack_weight(w2_words, w2_scales, "e4m3")
    wbu = unpack_weight(wb_words, wb_scales, "e4m3")
    sxu = unpack_weight(sx_words, sx_scales, "e5m2")
    wsu = unpack_weight(ws_words, ws_scales, "e4m3")
    xtidxg = xtu[:, idx]
    a = wu.T @ xtidxg
    xtidx2g = xtu[:, idx2]
    b = w2u.T @ xtidx2g
    pw = np.zeros((R, C))
    pw[:, idx3] = a
    pv = np.zeros((R, C))
    pv[:, idx4] = b
    hid = np.abs(pw[:, idx5] - pv[:, idx6])
    hidq = mxq(hid, 0, "e5m2")
    y = wbu.T @ hidq + wsu.T @ sxu
    return y

@@ -1,0 +1,198 @@
+from contextlib import ExitStack
+
+import concourse.mybir as mybir
+
+K, T, J, R, C, O, N, L = 512, 2048, 256, 512, 512, 256, 256, 512
+FLOPS = 2 * (2 * K * R * J + R * N * O + L * N * O)
+
+F32 = mybir.dt.float32
+BF16 = mybir.dt.bfloat16
+I32 = mybir.dt.int32
+U32 = mybir.dt.uint32
+U16 = mybir.dt.uint16
+U8 = mybir.dt.uint8
+E4M3 = mybir.dt.float8_e4m3fn_x4
+E5M2 = mybir.dt.float8_e5m2_x4
+E2M1 = mybir.dt.float4_e2m1fn_x4
+ACT = mybir.ActivationFunctionType
+ALU = mybir.AluOpType
+
+P = 128
+PACK = 4
+HALF = O // 2
+
+
+def tile_list_ahead_twoboards_skip_plain_kernel(
+    tc, xt_words, xt_scales, w_words, w_scales, w2_words, w2_scales, wb_words, wb_scales,
+    sx_words, sx_scales, ws_words, ws_scales, offs, offs2, offs3, offs4, offs5, offs6, out,
+):
+    nc = tc.nc
+    with ExitStack() as ctx:
+        keep = ctx.enter_context(tc.tile_pool(name="keep", bufs=1))
+        psum = ctx.enter_context(tc.psum_pool(name="psum", bufs=1))
+
+        def load_list(src, name):
+            t = keep.tile([P, J // 16], U16, name=name)
+            nc.sync.dma_start(t[:], src)
+            return t
+
+        def load_rows(plane, scales):
+            for q in range(4):
+                nc.sync.dma_start(plane[32 * q : 32 * q + 4, :].bitcast(I32), scales[0, 4 * q : 4 * q + 4, :].bitcast(I32))
+
+        def words_view(words):
+            return words[0].rearrange("p n t -> p (n t)").bitcast(I32)
+
+        xs = keep.tile([P, T], U8, name="xs", tag="slot_xs", align_bytes=64)
+        wsr = keep.tile([P, R], U8, name="wsr", align_bytes=64)
+        w2sr = keep.tile([P, R], U8, name="w2sr", align_bytes=64)
+        late = keep.tile([P, 3 * N], U8, name="late", align_bytes=64)
+        nc.vector.memset(xs[:].bitcast(I32), 0)
+        nc.gpsimd.memset(wsr[:].bitcast(I32), 0)
+        nc.gpsimd.memset(w2sr[:].bitcast(I32), 0)
+
+        xw = keep.tile([P, T], U16, name="xw", tag="slot_x", align_bytes=64)
+        wr = keep.tile([P, R], U32, name="wr", tag="slot_w", align_bytes=64)
+        nc.sync.dma_start(xw[:].bitcast(I32), xt_words[0].bitcast(I32))
+        nc.scalar.dma_start(wr[:].bitcast(I32), words_view(w_words))
+        l1 = load_list(offs, "l1")
+        load_rows(xs, xt_scales)
+        l2 = load_list(offs2, "l2")
+        load_rows(wsr, w_scales)
+        l3 = load_list(offs3, "l3")
+        w2r = keep.tile([P, R], U32, name="w2r", tag="slot_w2", align_bytes=64)
+        nc.sync.dma_start(w2r[:].bitcast(I32), words_view(w2_words))
+        load_rows(w2sr, w2_scales)
+        l4 = load_list(offs4, "l4")
+        l5 = load_list(offs5, "l5")
+        l6 = load_list(offs6, "l6")
+
+        pw = [keep.tile([P, C], F32, name="pw%d" % t) for t in range(PACK)]
+        pv = [keep.tile([P, C], F32, name="pv%d" % t) for t in range(PACK)]
+        for t in range(PACK):
+            nc.vector.memset(pw[t][:], 0.0)
+        for t in range(PACK):
+            nc.gpsimd.memset(pv[t][:], 0.0)
+        nc.gpsimd.memset(late[:].bitcast(I32), 0)
+        load_rows(late[:, 0:N], ws_scales)
+        load_rows(late[:, N : 2 * N], sx_scales)
+        load_rows(late[:, 2 * N : 3 * N], wb_scales)
+
+        def deal(eng, dst, src):
+            eng.tensor_copy(
+                dst[:].rearrange("p (t c i) -> p c t i", t=PACK, i=4),
+                src[:].rearrange("p (c i t) -> p c t i", t=PACK, i=4),
+            )
+
+        wp = keep.tile([P, R], U32, name="wp", align_bytes=64)
+        wsp = keep.tile([P, R], U8, name="wsp", align_bytes=64)
+        w2p = keep.tile([P, R], U32, name="w2p", align_bytes=64)
+        w2sp = keep.tile([P, R], U8, name="w2sp", align_bytes=64)
+        x1s = keep.tile([P, J], U8, name="x1s", align_bytes=64)
+        x2s = keep.tile([P, J], U8, name="x2s", align_bytes=64)
+        x1w = keep.tile([P, J], U16, name="x1w", align_bytes=64)
+        x2w = keep.tile([P, J], U16, name="x2w", align_bytes=64)
+
+        nc.vector.tensor_copy(x1s[:], xs[:].indirect(l1[:]))
+        deal(nc.vector, wp, wr)
+        nc.vector.tensor_copy(x1w[:], xw[:].indirect(l1[:]))
+        deal(nc.vector, wsp, wsr)
+        nc.vector.tensor_copy(x2s[:], xs[:].indirect(l2[:]))
+        nc.vector.tensor_copy(x2w[:], xw[:].indirect(l2[:]))
+
+        deal(nc.vector, w2p, w2r)
+        deal(nc.vector, w2sp, w2sr)
+
+        def first_stage(bank, wq, wsq, fmt, xq, xsq, t):
+            nc.tensor.matmul_mx(
+                out=bank[:, 0:J], lhsT=wq[:, t * P : (t + 1) * P].bitcast(fmt), lhsT_scale=wsq[:, t * P : (t + 1) * P],
+                rhs=xq[:].bitcast(E2M1), rhs_scale=xsq[:], start=True, stop=True,
+            )
+
+        pa = [psum.tile([P, 512], F32, name="pa%d" % t, tag="bank%d" % t) for t in range(PACK)]
+        pb = [psum.tile([P, 512], F32, name="pb%d" % t, tag="bank%d" % (PACK + t)) for t in range(PACK)]
+        for t in range(PACK):
+            first_stage(pa[t], wp, wsp, E5M2, x1w, x1s, t)
+        for t in range(PACK):
+            first_stage(pb[t], w2p, w2sp, E4M3, x2w, x2s, t)
+
+        wsw = keep.tile([P, N], U32, name="wsw", tag="slot_w", align_bytes=64)
+        sxw = keep.tile([P, O], U32, name="sxw", tag="slot_w2", align_bytes=64)
+        wbw = keep.tile([P, N], U32, name="wbw", tag="slot_x", align_bytes=64)
+        nc.sync.dma_start(wsw[:].bitcast(I32), words_view(ws_words))
+        nc.sync.dma_start(sxw[:].bitcast(I32), words_view(sx_words))
+        nc.sync.dma_start(wbw[:].bitcast(I32), words_view(wb_words))
+
+        a = [keep.tile([P, J], F32, name="a%d" % t) for t in range(PACK)]
+        b = [keep.tile([P, J], F32, name="b%d" % t) for t in range(PACK)]
+        g = [keep.tile([P, O], F32, name="g%d" % t) for t in range(PACK)]
+        d = [keep.tile([P, PACK, HALF], F32, name="d%d" % h) for h in range(2)]
+
+        def fetch(on_scalar, dst, bank):
+            if on_scalar:
+                nc.scalar.activation(dst[:], bank[:, 0:J], ACT.Copy)
+            else:
+                nc.vector.tensor_copy(dst[:], bank[:, 0:J])
+
+        def put(on_scalar, board, lst, src):
+            if on_scalar:
+                nc.scalar.activation(board[:].indirect(lst[:]), src[:], ACT.Copy)
+            else:
+                nc.vector.tensor_copy(board[:].indirect(lst[:]), src[:])
+
+        def look_w(t):
+            nc.scalar.activation(g[t][:], pw[t][:].indirect(l5[:]), ACT.Copy)
+
+        def look_v(t, h):
+            cols = HALF // 16
+            nc.vector.tensor_tensor(
+                d[h][:, t, :], pv[t][:].indirect(l6[:, h * cols : (h + 1) * cols]), g[t][:, h * HALF : (h + 1) * HALF], ALU.subtract
+            )
+
+        for u in range(2):
+            fetch(True, a[2 * u], pa[2 * u])
+            put(False, pw[2 * u], l3, a[2 * u])
+            fetch(True, a[2 * u + 1], pa[2 * u + 1])
+            put(True, pw[2 * u + 1], l3, a[2 * u + 1])
+        for t in range(PACK):
+            fetch(t % 2 == 1, b[t], pb[t])
+            put(t % 2 == 1, pv[t], l4, b[t])
+
+        py = [psum.tile([P, 512], F32, name="py%d" % h, tag="bank%d" % h) for h in range(2)]
+        for h in range(2):
+            for m in range(2):
+                nc.tensor.matmul_mx(
+                    out=py[h][:, m * HALF : (m + 1) * HALF], lhsT=wsw[:, m * P : (m + 1) * P].bitcast(E4M3),
+                    lhsT_scale=late[:, m * P : (m + 1) * P],
+                    rhs=sxw[:, h * HALF : (h + 1) * HALF].bitcast(E5M2), rhs_scale=late[:, N + h * HALF : N + (h + 1) * HALF],
+                    start=(m == 0), stop=False,
+                )
+
+        for t in range(PACK):
+            look_w(t)
+        for h in range(2):
+            for t in range(PACK):
+                look_v(t, h)
+
+        hid = [keep.tile([P, HALF * PACK], BF16, name="hid%d" % h, align_bytes=64) for h in range(2)]
+        hq = [keep.tile([P, HALF], U32, name="hq%d" % h, align_bytes=64) for h in range(2)]
+        hs = [keep.tile([P, HALF], U8, name="hs%d" % h, align_bytes=64) for h in range(2)]
+        y = [keep.tile([P, 2, HALF], F32, name="y%d" % h) for h in range(2)]
+        for h in range(2):
+            nc.scalar.activation(
+                hid[h][:].rearrange("p (c i t) -> p c t i", t=PACK, i=4),
+                d[h][:].rearrange("p t (c i) -> p c t i", i=4),
+                ACT.Abs,
+            )
+            nc.vector.quantize_mx(out=hq[h][:].bitcast(E5M2), scales=hs[h][:], in_=hid[h][:])
+            for m in range(2):
+                nc.tensor.matmul_mx(
+                    out=py[h][:, m * HALF : (m + 1) * HALF], lhsT=wbw[:, m * P : (m + 1) * P].bitcast(E4M3),
+                    lhsT_scale=late[:, 2 * N + m * P : 2 * N + (m + 1) * P],
+                    rhs=hq[h][:].bitcast(E5M2), rhs_scale=hs[h][:],
+                    start=False, stop=(m == 1),
+                )
+        nc.scalar.copy(y[0][:].rearrange("p m o -> p (m o)"), py[0][:, 0 : 2 * HALF])
+        nc.vector.tensor_copy(y[1][:].rearrange("p m o -> p (m o)"), py[1][:, 0 : 2 * HALF])
+        for h in range(2):
+            nc.sync.dma_start(out.rearrange("(m p) o -> p m o", p=P)[:, :, h * HALF : (h + 1) * HALF], y[h][:])

@@ -20,6 +20,7 @@ ALU = mybir.AluOpType
 P = 128
 PACK = 4
 HALF = O // 2
+LIVE = P - 16
 
 
 def tile_list_ahead_twoboards_skip_plain_kernel(
@@ -36,163 +37,180 @@ def tile_list_ahead_twoboards_skip_plain_kernel(
             nc.sync.dma_start(t[:], src)
             return t
 
-        def load_rows(plane, scales):
+        def load_rows(rows, scales):
+            nc.sync.dma_start(rows[LIVE:P, :].bitcast(I32), scales[0].bitcast(I32))
+
+        def carry(plane, rows, engines):
             for q in range(4):
-                nc.sync.dma_start(plane[32 * q : 32 * q + 4, :].bitcast(I32), scales[0, 4 * q : 4 * q + 4, :].bitcast(I32))
+                engines[q % 2].dma_start(
+                    plane[32 * q : 32 * q + 4, :].bitcast(I32), rows[LIVE + 4 * q : LIVE + 4 * q + 4, :].bitcast(I32)
+                )
 
         def words_view(words):
             return words[0].rearrange("p n t -> p (n t)").bitcast(I32)
 
         xs = keep.tile([P, T], U8, name="xs", tag="slot_xs", align_bytes=64)
-        wsr = keep.tile([P, R], U8, name="wsr", align_bytes=64)
-        w2sr = keep.tile([P, R], U8, name="w2sr", align_bytes=64)
-        late = keep.tile([P, 3 * N], U8, name="late", align_bytes=64)
-        nc.vector.memset(xs[:].bitcast(I32), 0)
-        nc.gpsimd.memset(wsr[:].bitcast(I32), 0)
-        nc.gpsimd.memset(w2sr[:].bitcast(I32), 0)
-
-        xw = keep.tile([P, T], U16, name="xw", tag="slot_x", align_bytes=64)
+        wsr = keep.tile([P, 2 * R], U8, name="wsr", align_bytes=64)
+        xw = keep.tile([P, T], U16, name="xw", align_bytes=64)
         wr = keep.tile([P, R], U32, name="wr", tag="slot_w", align_bytes=64)
-        nc.sync.dma_start(xw[:].bitcast(I32), xt_words[0].bitcast(I32))
-        nc.scalar.dma_start(wr[:].bitcast(I32), words_view(w_words))
-        l1 = load_list(offs, "l1")
         load_rows(xs, xt_scales)
+        nc.scalar.dma_start(xw[:].bitcast(I32), xt_words[0].bitcast(I32))
+        l1 = load_list(offs, "l1")
+        nc.scalar.dma_start(wr[:].bitcast(I32), words_view(w_words))
+        load_rows(wsr[:, 0:R], w_scales)
+        w2r = keep.tile([P, R], U32, name="w2r", align_bytes=64)
+        nc.scalar.dma_start(w2r[:].bitcast(I32), words_view(w2_words))
         l2 = load_list(offs2, "l2")
-        load_rows(wsr, w_scales)
+        load_rows(wsr[:, R : 2 * R], w2_scales)
         l3 = load_list(offs3, "l3")
-        w2r = keep.tile([P, R], U32, name="w2r", tag="slot_w2", align_bytes=64)
-        nc.sync.dma_start(w2r[:].bitcast(I32), words_view(w2_words))
-        load_rows(w2sr, w2_scales)
         l4 = load_list(offs4, "l4")
         l5 = load_list(offs5, "l5")
         l6 = load_list(offs6, "l6")
+        nc.vector.memset(xs[0:LIVE, :].bitcast(I32), 0)
+        nc.vector.memset(wsr[0:LIVE, :].bitcast(I32), 0)
 
+        plane_a = keep.tile([P, R + J], U8, name="plane_a", align_bytes=64)
+        plane_b = keep.tile([P, R + J], U8, name="plane_b", align_bytes=64)
+        late = keep.tile([P, 3 * N], U8, name="late", align_bytes=64)
+        for plane in (plane_a, plane_b, late):
+            nc.gpsimd.memset(plane[:].bitcast(I32), 0)
         pw = [keep.tile([P, C], F32, name="pw%d" % t) for t in range(PACK)]
         pv = [keep.tile([P, C], F32, name="pv%d" % t) for t in range(PACK)]
         for t in range(PACK):
             nc.vector.memset(pw[t][:], 0.0)
         for t in range(PACK):
             nc.gpsimd.memset(pv[t][:], 0.0)
-        nc.gpsimd.memset(late[:].bitcast(I32), 0)
-        load_rows(late[:, 0:N], ws_scales)
-        load_rows(late[:, N : 2 * N], sx_scales)
-        load_rows(late[:, 2 * N : 3 * N], wb_scales)
 
         def deal(eng, dst, src):
             eng.tensor_copy(
-                dst[:].rearrange("p (t c i) -> p c t i", t=PACK, i=4),
-                src[:].rearrange("p (c i t) -> p c t i", t=PACK, i=4),
+                dst.rearrange("p (t c i) -> p c t i", t=PACK, i=4),
+                src.rearrange("p (c i t) -> p c t i", t=PACK, i=4),
             )
 
         wp = keep.tile([P, R], U32, name="wp", align_bytes=64)
-        wsp = keep.tile([P, R], U8, name="wsp", align_bytes=64)
-        w2p = keep.tile([P, R], U32, name="w2p", align_bytes=64)
-        w2sp = keep.tile([P, R], U8, name="w2sp", align_bytes=64)
+        w2p = keep.tile([P, R], U32, name="w2p", tag="slot_w2p", align_bytes=64)
+        rows_a = keep.tile([P, R + J], U8, name="rows_a", align_bytes=64)
+        rows_b = keep.tile([P, R + J], U8, name="rows_b", align_bytes=64)
         x1s = keep.tile([P, J], U8, name="x1s", align_bytes=64)
         x2s = keep.tile([P, J], U8, name="x2s", align_bytes=64)
         x1w = keep.tile([P, J], U16, name="x1w", align_bytes=64)
         x2w = keep.tile([P, J], U16, name="x2w", align_bytes=64)
 
         nc.vector.tensor_copy(x1s[:], xs[:].indirect(l1[:]))
-        deal(nc.vector, wp, wr)
+        deal(nc.vector, rows_a[:, 0:R], wsr[:, 0:R])
+        nc.vector.tensor_copy(rows_a[:, R : R + J].bitcast(U32), x1s[:].bitcast(U32))
+        carry(plane_a, rows_a, (nc.sync, nc.sync))
         nc.vector.tensor_copy(x1w[:], xw[:].indirect(l1[:]))
-        deal(nc.vector, wsp, wsr)
+        deal(nc.vector, wp[:], wr[:])
         nc.vector.tensor_copy(x2s[:], xs[:].indirect(l2[:]))
+        deal(nc.vector, rows_b[:, 0:R], wsr[:, R : 2 * R])
+        nc.vector.tensor_copy(rows_b[:, R : R + J].bitcast(U32), x2s[:].bitcast(U32))
+        carry(plane_b, rows_b, (nc.sync, nc.sync))
         nc.vector.tensor_copy(x2w[:], xw[:].indirect(l2[:]))
+        deal(nc.vector, w2p[:], w2r[:])
 
-        deal(nc.vector, w2p, w2r)
-        deal(nc.vector, w2sp, w2sr)
+        rows_late = keep.tile([P, 3 * N], U8, name="rows_late", tag="slot_xs", align_bytes=64)
+        load_rows(rows_late[:, 0:N], ws_scales)
+        load_rows(rows_late[:, N : 2 * N], sx_scales)
+        load_rows(rows_late[:, 2 * N : 3 * N], wb_scales)
+        carry(late, rows_late, (nc.sync, nc.sync))
 
-        def first_stage(bank, wq, wsq, fmt, xq, xsq, t):
+        def first_stage(bank, wq, fmt, xq, plane, t):
             nc.tensor.matmul_mx(
-                out=bank[:, 0:J], lhsT=wq[:, t * P : (t + 1) * P].bitcast(fmt), lhsT_scale=wsq[:, t * P : (t + 1) * P],
-                rhs=xq[:].bitcast(E2M1), rhs_scale=xsq[:], start=True, stop=True,
+                out=bank, lhsT=wq[:, t * P : (t + 1) * P].bitcast(fmt), lhsT_scale=plane[:, t * P : (t + 1) * P],
+                rhs=xq[:].bitcast(E2M1), rhs_scale=plane[:, R : R + J], start=True, stop=True,
             )
 
         pa = [psum.tile([P, 512], F32, name="pa%d" % t, tag="bank%d" % t) for t in range(PACK)]
-        pb = [psum.tile([P, 512], F32, name="pb%d" % t, tag="bank%d" % (PACK + t)) for t in range(PACK)]
+        pb = [psum.tile([P, 2, J], F32, name="pb%d" % e, tag="bank%d" % (PACK + e)) for e in range(2)]
         for t in range(PACK):
-            first_stage(pa[t], wp, wsp, E5M2, x1w, x1s, t)
-        for t in range(PACK):
-            first_stage(pb[t], w2p, w2sp, E4M3, x2w, x2s, t)
+            first_stage(pa[t][:, 0:J], wp, E5M2, x1w, plane_a, t)
+        for t in (0, 2, 1, 3):
+            first_stage(pb[t % 2][:, t // 2, :], w2p, E4M3, x2w, plane_b, t)
 
-        wsw = keep.tile([P, N], U32, name="wsw", tag="slot_w", align_bytes=64)
-        sxw = keep.tile([P, O], U32, name="sxw", tag="slot_w2", align_bytes=64)
-        wbw = keep.tile([P, N], U32, name="wbw", tag="slot_x", align_bytes=64)
+        skip = keep.tile([P, N + O], U32, name="skip", tag="slot_w2p", align_bytes=64)
+        wsw = skip[:, 0:N]
+        sxw = skip[:, N : N + O]
+        wbw = keep.tile([P, N], U32, name="wbw", tag="slot_w", align_bytes=64)
         nc.sync.dma_start(wsw[:].bitcast(I32), words_view(ws_words))
         nc.sync.dma_start(sxw[:].bitcast(I32), words_view(sx_words))
         nc.sync.dma_start(wbw[:].bitcast(I32), words_view(wb_words))
 
         a = [keep.tile([P, J], F32, name="a%d" % t) for t in range(PACK)]
-        b = [keep.tile([P, J], F32, name="b%d" % t) for t in range(PACK)]
+        b = [keep.tile([P, 2, J], F32, name="b%d" % e) for e in range(2)]
         g = [keep.tile([P, O], F32, name="g%d" % t) for t in range(PACK)]
-        d = [keep.tile([P, PACK, HALF], F32, name="d%d" % h) for h in range(2)]
+        d_lo = keep.tile([P, 2, O], F32, name="d_lo")
+        d_hi = [keep.tile([P, 2, HALF], F32, name="d_hi%d" % h) for h in range(2)]
 
         def fetch(on_scalar, dst, bank):
             if on_scalar:
-                nc.scalar.activation(dst[:], bank[:, 0:J], ACT.Copy)
+                nc.scalar.activation(dst, bank, ACT.Copy)
             else:
-                nc.vector.tensor_copy(dst[:], bank[:, 0:J])
+                nc.vector.tensor_copy(dst, bank)
 
         def put(on_scalar, board, lst, src):
             if on_scalar:
-                nc.scalar.activation(board[:].indirect(lst[:]), src[:], ACT.Copy)
+                nc.scalar.activation(board[:].indirect(lst[:]), src, ACT.Copy)
             else:
-                nc.vector.tensor_copy(board[:].indirect(lst[:]), src[:])
+                nc.vector.tensor_copy(board[:].indirect(lst[:]), src)
 
         def look_w(t):
             nc.scalar.activation(g[t][:], pw[t][:].indirect(l5[:]), ACT.Copy)
 
-        def look_v(t, h):
-            cols = HALF // 16
-            nc.vector.tensor_tensor(
-                d[h][:, t, :], pv[t][:].indirect(l6[:, h * cols : (h + 1) * cols]), g[t][:, h * HALF : (h + 1) * HALF], ALU.subtract
-            )
+        def look_v(dst, t, lo, hi):
+            nc.vector.tensor_tensor(dst, pv[t][:].indirect(l6[:, lo // 16 : hi // 16]), g[t][:, lo:hi], ALU.subtract)
 
-        for u in range(2):
-            fetch(True, a[2 * u], pa[2 * u])
-            put(False, pw[2 * u], l3, a[2 * u])
-            fetch(True, a[2 * u + 1], pa[2 * u + 1])
-            put(True, pw[2 * u + 1], l3, a[2 * u + 1])
         for t in range(PACK):
-            fetch(t % 2 == 1, b[t], pb[t])
-            put(t % 2 == 1, pv[t], l4, b[t])
+            fetch(t % 2 == 1, a[t][:], pa[t][:, 0:J])
+            put(t % 2 == 1, pw[t], l3, a[t][:])
+        for e in range(2):
+            fetch(e == 1, b[e][:], pb[e][:])
+        for t in range(PACK):
+            put(t % 2 == 1, pv[t], l4, b[t % 2][:, t // 2, :])
 
-        py = [psum.tile([P, 512], F32, name="py%d" % h, tag="bank%d" % h) for h in range(2)]
+        py0 = psum.tile([P, 512], F32, name="py0", tag="bank0")
+        py1 = [psum.tile([P, 512], F32, name="py1%d" % m, tag="bank%d" % (1 + m)) for m in range(2)]
+
+        def sums(h, m):
+            return py0[:, m * HALF : (m + 1) * HALF] if h == 0 else py1[m][:, 0:HALF]
+
         for h in range(2):
             for m in range(2):
                 nc.tensor.matmul_mx(
-                    out=py[h][:, m * HALF : (m + 1) * HALF], lhsT=wsw[:, m * P : (m + 1) * P].bitcast(E4M3),
+                    out=sums(h, m), lhsT=wsw[:, m * P : (m + 1) * P].bitcast(E4M3),
                     lhsT_scale=late[:, m * P : (m + 1) * P],
                     rhs=sxw[:, h * HALF : (h + 1) * HALF].bitcast(E5M2), rhs_scale=late[:, N + h * HALF : N + (h + 1) * HALF],
-                    start=(m == 0), stop=False,
+                    start=(h == 1 or m == 0), stop=False,
                 )
+
+        hid = [keep.tile([P, HALF, PACK], BF16, name="hid%d" % h, align_bytes=64) for h in range(2)]
+        hq = [keep.tile([P, HALF], U32, name="hq%d" % h, align_bytes=64) for h in range(2)]
+        hs = [keep.tile([P, HALF], U8, name="hs%d" % h, align_bytes=64) for h in range(2)]
+        y0 = keep.tile([P, 2, HALF], F32, name="y0")
+        y1 = [keep.tile([P, HALF], F32, name="y1%d" % m) for m in range(2)]
 
         for t in range(PACK):
             look_w(t)
+        for t in range(2):
+            look_v(d_lo[:, t, :], t, 0, O)
         for h in range(2):
-            for t in range(PACK):
-                look_v(t, h)
-
-        hid = [keep.tile([P, HALF * PACK], BF16, name="hid%d" % h, align_bytes=64) for h in range(2)]
-        hq = [keep.tile([P, HALF], U32, name="hq%d" % h, align_bytes=64) for h in range(2)]
-        hs = [keep.tile([P, HALF], U8, name="hs%d" % h, align_bytes=64) for h in range(2)]
-        y = [keep.tile([P, 2, HALF], F32, name="y%d" % h) for h in range(2)]
+            for t in range(2):
+                look_v(d_hi[h][:, t, :], 2 + t, h * HALF, (h + 1) * HALF)
         for h in range(2):
-            nc.scalar.activation(
-                hid[h][:].rearrange("p (c i t) -> p c t i", t=PACK, i=4),
-                d[h][:].rearrange("p t (c i) -> p c t i", i=4),
-                ACT.Abs,
-            )
-            nc.vector.quantize_mx(out=hq[h][:].bitcast(E5M2), scales=hs[h][:], in_=hid[h][:])
+            nc.scalar.activation(hid[h][:, :, 0:2], d_lo[:, :, h * HALF : (h + 1) * HALF].rearrange("p t o -> p o t"), ACT.Abs)
+        for h in range(2):
+            nc.scalar.activation(hid[h][:, :, 2:4], d_hi[h][:].rearrange("p t o -> p o t"), ACT.Abs)
+            nc.vector.quantize_mx(out=hq[h][:].bitcast(E5M2), scales=hs[h][:], in_=hid[h][:].rearrange("p o t -> p (o t)"))
             for m in range(2):
                 nc.tensor.matmul_mx(
-                    out=py[h][:, m * HALF : (m + 1) * HALF], lhsT=wbw[:, m * P : (m + 1) * P].bitcast(E4M3),
+                    out=sums(h, m), lhsT=wbw[:, m * P : (m + 1) * P].bitcast(E4M3),
                     lhsT_scale=late[:, 2 * N + m * P : 2 * N + (m + 1) * P],
                     rhs=hq[h][:].bitcast(E5M2), rhs_scale=hs[h][:],
-                    start=False, stop=(m == 1),
+                    start=False, stop=(h == 1 or m == 1),
                 )
-        nc.scalar.copy(y[0][:].rearrange("p m o -> p (m o)"), py[0][:, 0 : 2 * HALF])
-        nc.vector.tensor_copy(y[1][:].rearrange("p m o -> p (m o)"), py[1][:, 0 : 2 * HALF])
-        for h in range(2):
-            nc.sync.dma_start(out.rearrange("(m p) o -> p m o", p=P)[:, :, h * HALF : (h + 1) * HALF], y[h][:])
+        nc.scalar.copy(y0[:].rearrange("p m o -> p (m o)"), py0[:, 0 : 2 * HALF])
+        nc.sync.dma_start(out.rearrange("(m p) o -> p m o", p=P)[:, :, 0:HALF], y0[:])
+        nc.scalar.copy(y1[0][:], sums(1, 0))
+        nc.vector.tensor_copy(y1[1][:], sums(1, 1))
+        nc.scalar.dma_start(out[0:P, HALF:O], y1[0][:])
+        nc.sync.dma_start(out[P:N, HALF:O], y1[1][:])

@@ -30,6 +30,7 @@ def tile_list_ahead_twoboards_skip_plain_kernel(
     nc = tc.nc
     with ExitStack() as ctx:
         keep = ctx.enter_context(tc.tile_pool(name="keep", bufs=1))
+        reuse = ctx.enter_context(tc.tile_pool(name="reuse", bufs=1))
         psum = ctx.enter_context(tc.psum_pool(name="psum", bufs=1))
 
         def load_list(src, name):
@@ -49,19 +50,19 @@ def tile_list_ahead_twoboards_skip_plain_kernel(
         def words_view(words):
             return words[0].rearrange("p n t -> p (n t)").bitcast(I32)
 
-        xs = keep.tile([P, T], U8, name="xs", tag="slot_xs", align_bytes=64)
+        xs = keep.tile([P, T], U8, name="xs", align_bytes=64)
         wsr = keep.tile([P, 2 * R], U8, name="wsr", align_bytes=64)
-        xw = keep.tile([P, T], U16, name="xw", align_bytes=64)
-        wr = keep.tile([P, R], U32, name="wr", tag="slot_w", align_bytes=64)
+        xw = reuse.tile([P, T], U16, name="xw", offset=0)
+        wr = keep.tile([P, R], U32, name="wr", align_bytes=64)
+        w2r = keep.tile([P, R], U32, name="w2r", tag="slot_w2r", align_bytes=64)
         load_rows(xs, xt_scales)
-        nc.scalar.dma_start(xw[:].bitcast(I32), xt_words[0].bitcast(I32))
         l1 = load_list(offs, "l1")
-        nc.scalar.dma_start(wr[:].bitcast(I32), words_view(w_words))
         load_rows(wsr[:, 0:R], w_scales)
-        w2r = keep.tile([P, R], U32, name="w2r", align_bytes=64)
-        nc.scalar.dma_start(w2r[:].bitcast(I32), words_view(w2_words))
+        nc.sync.dma_start(xw[:].bitcast(I32), xt_words[0].bitcast(I32))
+        nc.sync.dma_start(wr[:].bitcast(I32), words_view(w_words))
         l2 = load_list(offs2, "l2")
         load_rows(wsr[:, R : 2 * R], w2_scales)
+        nc.sync.dma_start(w2r[:].bitcast(I32), words_view(w2_words))
         l3 = load_list(offs3, "l3")
         l4 = load_list(offs4, "l4")
         l5 = load_list(offs5, "l5")
@@ -72,14 +73,9 @@ def tile_list_ahead_twoboards_skip_plain_kernel(
         plane_a = keep.tile([P, R + J], U8, name="plane_a", align_bytes=64)
         plane_b = keep.tile([P, R + J], U8, name="plane_b", align_bytes=64)
         late = keep.tile([P, 3 * N], U8, name="late", align_bytes=64)
-        for plane in (plane_a, plane_b, late):
-            nc.gpsimd.memset(plane[:].bitcast(I32), 0)
         pw = [keep.tile([P, C], F32, name="pw%d" % t) for t in range(PACK)]
-        pv = [keep.tile([P, C], F32, name="pv%d" % t) for t in range(PACK)]
         for t in range(PACK):
             nc.vector.memset(pw[t][:], 0.0)
-        for t in range(PACK):
-            nc.gpsimd.memset(pv[t][:], 0.0)
 
         def deal(eng, dst, src):
             eng.tensor_copy(
@@ -87,29 +83,29 @@ def tile_list_ahead_twoboards_skip_plain_kernel(
                 src.rearrange("p (c i t) -> p c t i", t=PACK, i=4),
             )
 
-        wp = keep.tile([P, R], U32, name="wp", align_bytes=64)
+        wp = keep.tile([P, R], U32, name="wp", tag="slot_w", align_bytes=64)
         w2p = keep.tile([P, R], U32, name="w2p", tag="slot_w2p", align_bytes=64)
         rows_a = keep.tile([P, R + J], U8, name="rows_a", align_bytes=64)
-        rows_b = keep.tile([P, R + J], U8, name="rows_b", align_bytes=64)
+        rows_b = keep.tile([P, R + J], U8, name="rows_b", tag="slot_rows", align_bytes=64)
         x1s = keep.tile([P, J], U8, name="x1s", align_bytes=64)
         x2s = keep.tile([P, J], U8, name="x2s", align_bytes=64)
-        x1w = keep.tile([P, J], U16, name="x1w", align_bytes=64)
-        x2w = keep.tile([P, J], U16, name="x2w", align_bytes=64)
+        x1w = keep.tile([P, J], U16, name="x1w", tag="slot_x1w", align_bytes=64)
+        x2w = keep.tile([P, J], U16, name="x2w", tag="slot_x2w", align_bytes=64)
 
         nc.vector.tensor_copy(x1s[:], xs[:].indirect(l1[:]))
         deal(nc.vector, rows_a[:, 0:R], wsr[:, 0:R])
         nc.vector.tensor_copy(rows_a[:, R : R + J].bitcast(U32), x1s[:].bitcast(U32))
-        carry(plane_a, rows_a, (nc.sync, nc.sync))
+        carry(plane_a, rows_a, (nc.scalar, nc.scalar))
         nc.vector.tensor_copy(x1w[:], xw[:].indirect(l1[:]))
         deal(nc.vector, wp[:], wr[:])
         nc.vector.tensor_copy(x2s[:], xs[:].indirect(l2[:]))
         deal(nc.vector, rows_b[:, 0:R], wsr[:, R : 2 * R])
         nc.vector.tensor_copy(rows_b[:, R : R + J].bitcast(U32), x2s[:].bitcast(U32))
         carry(plane_b, rows_b, (nc.sync, nc.sync))
-        nc.vector.tensor_copy(x2w[:], xw[:].indirect(l2[:]))
         deal(nc.vector, w2p[:], w2r[:])
+        nc.vector.tensor_copy(x2w[:], xw[:].indirect(l2[:]))
 
-        rows_late = keep.tile([P, 3 * N], U8, name="rows_late", tag="slot_xs", align_bytes=64)
+        rows_late = keep.tile([P, 3 * N], U8, name="rows_late", tag="slot_rows", align_bytes=64)
         load_rows(rows_late[:, 0:N], ws_scales)
         load_rows(rows_late[:, N : 2 * N], sx_scales)
         load_rows(rows_late[:, 2 * N : 3 * N], wb_scales)
@@ -128,15 +124,23 @@ def tile_list_ahead_twoboards_skip_plain_kernel(
         for t in (0, 2, 1, 3):
             first_stage(pb[t % 2][:, t // 2, :], w2p, E4M3, x2w, plane_b, t)
 
-        skip = keep.tile([P, N + O], U32, name="skip", tag="slot_w2p", align_bytes=64)
+        skip = keep.tile([P, N + O], U32, name="skip", tag="slot_x2w", align_bytes=64)
         wsw = skip[:, 0:N]
         sxw = skip[:, N : N + O]
-        wbw = keep.tile([P, N], U32, name="wbw", tag="slot_w", align_bytes=64)
+        wbw = keep.tile([P, N], U32, name="wbw", tag="slot_x1w", align_bytes=64)
         nc.sync.dma_start(wsw[:].bitcast(I32), words_view(ws_words))
         nc.sync.dma_start(sxw[:].bitcast(I32), words_view(sx_words))
         nc.sync.dma_start(wbw[:].bitcast(I32), words_view(wb_words))
 
-        a = [keep.tile([P, J], F32, name="a%d" % t) for t in range(PACK)]
+        pv = [
+            keep.tile([P, C], F32, name="pv0", tag="slot_w", align_bytes=64),
+            reuse.tile([P, C], F32, name="pv1", offset=0),
+            reuse.tile([P, C], F32, name="pv2", offset=4 * C),
+            keep.tile([P, C], F32, name="pv3", tag="slot_w2p", align_bytes=64),
+        ]
+        for t in range(PACK):
+            nc.gpsimd.memset(pv[t][:], 0.0)
+        a = [keep.tile([P, J], F32, name="a%d" % t, tag="slot_w2r" if t == 2 else "a%d" % t, align_bytes=64) for t in range(PACK)]
         b = [keep.tile([P, 2, J], F32, name="b%d" % e) for e in range(2)]
         g = [keep.tile([P, O], F32, name="g%d" % t) for t in range(PACK)]
         d_lo = keep.tile([P, 2, O], F32, name="d_lo")

@@ -19,8 +19,14 @@ ALU = mybir.AluOpType
 
 P = 128
 PACK = 4
+GROUP = 16
+QUADS = 4
+BANK = 512
+LINE = 4
 HALF = O // 2
 LIVE = P - 16
+VECTOR_SLICES = (0, 1)
+SCALAR_SLICES = (2, 3)
 
 
 def tile_list_ahead_twoboards_skip_plain_kernel(
@@ -34,21 +40,27 @@ def tile_list_ahead_twoboards_skip_plain_kernel(
         psum = ctx.enter_context(tc.psum_pool(name="psum", bufs=1))
 
         def load_list(src, name):
-            t = keep.tile([P, J // 16], U16, name=name)
-            nc.sync.dma_start(t[:], src)
-            return t
+            lst = keep.tile([P, J // GROUP], U16, name=name)
+            nc.sync.dma_start(lst[:], src)
+            return lst
 
         def load_rows(rows, scales):
             nc.sync.dma_start(rows[LIVE:P, :].bitcast(I32), scales[0].bitcast(I32))
 
-        def carry(plane, rows, engines):
-            for q in range(4):
-                engines[q % 2].dma_start(
+        def carry(queue, plane, rows):
+            for q in range(QUADS):
+                queue.dma_start(
                     plane[32 * q : 32 * q + 4, :].bitcast(I32), rows[LIVE + 4 * q : LIVE + 4 * q + 4, :].bitcast(I32)
                 )
 
         def words_view(words):
             return words[0].rearrange("p n t -> p (n t)").bitcast(I32)
+
+        def deal(dst, src):
+            nc.vector.tensor_copy(
+                dst.rearrange("p (t c i) -> p c t i", t=PACK, i=LINE),
+                src.rearrange("p (c i t) -> p c t i", t=PACK, i=LINE),
+            )
 
         xs = keep.tile([P, T], U8, name="xs", align_bytes=64)
         wsr = keep.tile([P, 2 * R], U8, name="wsr", align_bytes=64)
@@ -77,12 +89,6 @@ def tile_list_ahead_twoboards_skip_plain_kernel(
         for t in range(PACK):
             nc.vector.memset(pw[t][:], 0.0)
 
-        def deal(eng, dst, src):
-            eng.tensor_copy(
-                dst.rearrange("p (t c i) -> p c t i", t=PACK, i=4),
-                src.rearrange("p (c i t) -> p c t i", t=PACK, i=4),
-            )
-
         wp = keep.tile([P, R], U32, name="wp", tag="slot_w", align_bytes=64)
         w2p = keep.tile([P, R], U32, name="w2p", tag="slot_w2p", align_bytes=64)
         rows_a = keep.tile([P, R + J], U8, name="rows_a", align_bytes=64)
@@ -93,23 +99,23 @@ def tile_list_ahead_twoboards_skip_plain_kernel(
         x2w = keep.tile([P, J], U16, name="x2w", tag="slot_x2w", align_bytes=64)
 
         nc.vector.tensor_copy(x1s[:], xs[:].indirect(l1[:]))
-        deal(nc.vector, rows_a[:, 0:R], wsr[:, 0:R])
+        deal(rows_a[:, 0:R], wsr[:, 0:R])
         nc.vector.tensor_copy(rows_a[:, R : R + J].bitcast(U32), x1s[:].bitcast(U32))
-        carry(plane_a, rows_a, (nc.scalar, nc.scalar))
+        carry(nc.scalar, plane_a, rows_a)
         nc.vector.tensor_copy(x1w[:], xw[:].indirect(l1[:]))
-        deal(nc.vector, wp[:], wr[:])
+        deal(wp[:], wr[:])
         nc.vector.tensor_copy(x2s[:], xs[:].indirect(l2[:]))
-        deal(nc.vector, rows_b[:, 0:R], wsr[:, R : 2 * R])
+        deal(rows_b[:, 0:R], wsr[:, R : 2 * R])
         nc.vector.tensor_copy(rows_b[:, R : R + J].bitcast(U32), x2s[:].bitcast(U32))
-        carry(plane_b, rows_b, (nc.sync, nc.sync))
-        deal(nc.vector, w2p[:], w2r[:])
+        carry(nc.sync, plane_b, rows_b)
+        deal(w2p[:], w2r[:])
         nc.vector.tensor_copy(x2w[:], xw[:].indirect(l2[:]))
 
         rows_late = keep.tile([P, 3 * N], U8, name="rows_late", tag="slot_rows", align_bytes=64)
         load_rows(rows_late[:, 0:N], ws_scales)
         load_rows(rows_late[:, N : 2 * N], sx_scales)
         load_rows(rows_late[:, 2 * N : 3 * N], wb_scales)
-        carry(late, rows_late, (nc.sync, nc.sync))
+        carry(nc.sync, late, rows_late)
 
         def first_stage(bank, wq, fmt, xq, plane, t):
             nc.tensor.matmul_mx(
@@ -117,12 +123,12 @@ def tile_list_ahead_twoboards_skip_plain_kernel(
                 rhs=xq[:].bitcast(E2M1), rhs_scale=plane[:, R : R + J], start=True, stop=True,
             )
 
-        pa = [psum.tile([P, 512], F32, name="pa%d" % t, tag="bank%d" % t) for t in range(PACK)]
+        pa = [psum.tile([P, BANK], F32, name="pa%d" % t, tag="bank%d" % t) for t in range(PACK)]
         pb = [psum.tile([P, 2, J], F32, name="pb%d" % e, tag="bank%d" % (PACK + e)) for e in range(2)]
-        for t in range(PACK):
+        for t in SCALAR_SLICES + VECTOR_SLICES:
             first_stage(pa[t][:, 0:J], wp, E5M2, x1w, plane_a, t)
-        for t in (0, 2, 1, 3):
-            first_stage(pb[t % 2][:, t // 2, :], w2p, E4M3, x2w, plane_b, t)
+        for t in range(PACK):
+            first_stage(pb[t // 2][:, t % 2, :], w2p, E4M3, x2w, plane_b, t)
 
         skip = keep.tile([P, N + O], U32, name="skip", tag="slot_x2w", align_bytes=64)
         wsw = skip[:, 0:N]
@@ -133,47 +139,50 @@ def tile_list_ahead_twoboards_skip_plain_kernel(
         nc.sync.dma_start(wbw[:].bitcast(I32), words_view(wb_words))
 
         pv = [
-            keep.tile([P, C], F32, name="pv0", tag="slot_w", align_bytes=64),
-            reuse.tile([P, C], F32, name="pv1", offset=0),
+            reuse.tile([P, C], F32, name="pv0", offset=0),
+            keep.tile([P, C], F32, name="pv1", tag="slot_w", align_bytes=64),
             reuse.tile([P, C], F32, name="pv2", offset=4 * C),
             keep.tile([P, C], F32, name="pv3", tag="slot_w2p", align_bytes=64),
         ]
         for t in range(PACK):
             nc.gpsimd.memset(pv[t][:], 0.0)
-        a = [keep.tile([P, J], F32, name="a%d" % t, tag="slot_w2r" if t == 2 else "a%d" % t, align_bytes=64) for t in range(PACK)]
-        b = [keep.tile([P, 2, J], F32, name="b%d" % e) for e in range(2)]
+        a = [
+            keep.tile([P, J], F32, name="a%d" % t, tag="slot_w2r" if t == VECTOR_SLICES[-1] else "a%d" % t, align_bytes=64)
+            for t in range(PACK)
+        ]
+        b = [keep.tile([P, J], F32, name="b%d" % t) for t in range(PACK)]
         g = [keep.tile([P, O], F32, name="g%d" % t) for t in range(PACK)]
         d_lo = keep.tile([P, 2, O], F32, name="d_lo")
         d_hi = [keep.tile([P, 2, HALF], F32, name="d_hi%d" % h) for h in range(2)]
 
-        def fetch(on_scalar, dst, bank):
-            if on_scalar:
+        def fetch(t, dst, bank):
+            if t in SCALAR_SLICES:
                 nc.scalar.activation(dst, bank, ACT.Copy)
             else:
                 nc.vector.tensor_copy(dst, bank)
 
-        def put(on_scalar, board, lst, src):
-            if on_scalar:
-                nc.scalar.activation(board[:].indirect(lst[:]), src, ACT.Copy)
+        def put(t, board, lst, src):
+            if t in SCALAR_SLICES:
+                nc.scalar.activation(board[t][:].indirect(lst[:]), src[t][:], ACT.Copy)
             else:
-                nc.vector.tensor_copy(board[:].indirect(lst[:]), src)
-
-        def look_w(t):
-            nc.scalar.activation(g[t][:], pw[t][:].indirect(l5[:]), ACT.Copy)
+                nc.vector.tensor_copy(board[t][:].indirect(lst[:]), src[t][:])
 
         def look_v(dst, t, lo, hi):
-            nc.vector.tensor_tensor(dst, pv[t][:].indirect(l6[:, lo // 16 : hi // 16]), g[t][:, lo:hi], ALU.subtract)
+            nc.vector.tensor_tensor(dst, pv[t][:].indirect(l6[:, lo // GROUP : hi // GROUP]), g[t][:, lo:hi], ALU.subtract)
 
+        for t in SCALAR_SLICES + VECTOR_SLICES:
+            fetch(t, a[t][:], pa[t][:, 0:J])
+        for u in range(2):
+            put(SCALAR_SLICES[u], pw, l3, a)
+            put(VECTOR_SLICES[u], pw, l3, a)
         for t in range(PACK):
-            fetch(t % 2 == 1, a[t][:], pa[t][:, 0:J])
-            put(t % 2 == 1, pw[t], l3, a[t][:])
-        for e in range(2):
-            fetch(e == 1, b[e][:], pb[e][:])
-        for t in range(PACK):
-            put(t % 2 == 1, pv[t], l4, b[t % 2][:, t // 2, :])
+            fetch(t, b[t][:], pb[t // 2][:, t % 2, :])
+        for u in range(2):
+            put(VECTOR_SLICES[u], pv, l4, b)
+            put(SCALAR_SLICES[u], pv, l4, b)
 
-        py0 = psum.tile([P, 512], F32, name="py0", tag="bank0")
-        py1 = [psum.tile([P, 512], F32, name="py1%d" % m, tag="bank%d" % (1 + m)) for m in range(2)]
+        py0 = psum.tile([P, BANK], F32, name="py0", tag="bank0")
+        py1 = [psum.tile([P, BANK], F32, name="py1%d" % m, tag="bank%d" % (1 + m)) for m in range(2)]
 
         def sums(h, m):
             return py0[:, m * HALF : (m + 1) * HALF] if h == 0 else py1[m][:, 0:HALF]
@@ -194,12 +203,12 @@ def tile_list_ahead_twoboards_skip_plain_kernel(
         y1 = [keep.tile([P, HALF], F32, name="y1%d" % m) for m in range(2)]
 
         for t in range(PACK):
-            look_w(t)
-        for t in range(2):
-            look_v(d_lo[:, t, :], t, 0, O)
-        for h in range(2):
-            for t in range(2):
-                look_v(d_hi[h][:, t, :], 2 + t, h * HALF, (h + 1) * HALF)
+            nc.scalar.activation(g[t][:], pw[t][:].indirect(l5[:]), ACT.Copy)
+        for u in range(2):
+            look_v(d_lo[:, u, :], u, 0, O)
+        for u in range(2):
+            for h in range(2):
+                look_v(d_hi[h][:, u, :], 2 + u, h * HALF, (h + 1) * HALF)
         for h in range(2):
             nc.scalar.activation(hid[h][:, :, 0:2], d_lo[:, :, h * HALF : (h + 1) * HALF].rearrange("p t o -> p o t"), ACT.Abs)
         for h in range(2):

from contextlib import ExitStack

import concourse.mybir as mybir

K, T, J, R, C, O, N, L = 512, 2048, 256, 512, 512, 256, 256, 512
FLOPS = 2 * (2 * K * R * J + R * N * O + L * N * O)

F32 = mybir.dt.float32
BF16 = mybir.dt.bfloat16
I32 = mybir.dt.int32
U32 = mybir.dt.uint32
U16 = mybir.dt.uint16
U8 = mybir.dt.uint8
E4M3 = mybir.dt.float8_e4m3fn_x4
E5M2 = mybir.dt.float8_e5m2_x4
E2M1 = mybir.dt.float4_e2m1fn_x4
ACT = mybir.ActivationFunctionType
ALU = mybir.AluOpType

P = 128
PACK = 4
GROUP = 16
QUADS = 4
BANK = 512
LINE = 4
HALF = O // 2
LIVE = P - 16
VECTOR_SLICES = (0, 1)
SCALAR_SLICES = (2, 3)


def tile_list_ahead_twoboards_skip_plain_kernel(
    tc, xt_words, xt_scales, w_words, w_scales, w2_words, w2_scales, wb_words, wb_scales,
    sx_words, sx_scales, ws_words, ws_scales, offs, offs2, offs3, offs4, offs5, offs6, out,
):
    nc = tc.nc
    with ExitStack() as ctx:
        keep = ctx.enter_context(tc.tile_pool(name="keep", bufs=1))
        reuse = ctx.enter_context(tc.tile_pool(name="reuse", bufs=1))
        psum = ctx.enter_context(tc.psum_pool(name="psum", bufs=1))

        def load_list(src, name):
            lst = keep.tile([P, J // GROUP], U16, name=name)
            nc.sync.dma_start(lst[:], src)
            return lst

        def load_rows(rows, scales):
            nc.sync.dma_start(rows[LIVE:P, :].bitcast(I32), scales[0].bitcast(I32))

        def carry(queue, plane, rows):
            for q in range(QUADS):
                queue.dma_start(
                    plane[32 * q : 32 * q + 4, :].bitcast(I32), rows[LIVE + 4 * q : LIVE + 4 * q + 4, :].bitcast(I32)
                )

        def words_view(words):
            return words[0].rearrange("p n t -> p (n t)").bitcast(I32)

        def deal(dst, src):
            nc.vector.tensor_copy(
                dst.rearrange("p (t c i) -> p c t i", t=PACK, i=LINE),
                src.rearrange("p (c i t) -> p c t i", t=PACK, i=LINE),
            )

        xs = keep.tile([P, T], U8, name="xs", align_bytes=64)
        wsr = keep.tile([P, 2 * R], U8, name="wsr", align_bytes=64)
        xw = reuse.tile([P, T], U16, name="xw", offset=0)
        wr = keep.tile([P, R], U32, name="wr", align_bytes=64)
        w2r = keep.tile([P, R], U32, name="w2r", tag="slot_w2r", align_bytes=64)
        load_rows(xs, xt_scales)
        l1 = load_list(offs, "l1")
        load_rows(wsr[:, 0:R], w_scales)
        nc.sync.dma_start(xw[:].bitcast(I32), xt_words[0].bitcast(I32))
        nc.sync.dma_start(wr[:].bitcast(I32), words_view(w_words))
        l2 = load_list(offs2, "l2")
        load_rows(wsr[:, R : 2 * R], w2_scales)
        nc.sync.dma_start(w2r[:].bitcast(I32), words_view(w2_words))
        l3 = load_list(offs3, "l3")
        l4 = load_list(offs4, "l4")
        l5 = load_list(offs5, "l5")
        l6 = load_list(offs6, "l6")
        nc.vector.memset(xs[0:LIVE, :].bitcast(I32), 0)
        nc.vector.memset(wsr[0:LIVE, :].bitcast(I32), 0)

        plane_a = keep.tile([P, R + J], U8, name="plane_a", align_bytes=64)
        plane_b = keep.tile([P, R + J], U8, name="plane_b", align_bytes=64)
        late = keep.tile([P, 3 * N], U8, name="late", align_bytes=64)
        pw = [keep.tile([P, C], F32, name="pw%d" % t) for t in range(PACK)]
        for t in range(PACK):
            nc.vector.memset(pw[t][:], 0.0)

        wp = keep.tile([P, R], U32, name="wp", tag="slot_w", align_bytes=64)
        w2p = keep.tile([P, R], U32, name="w2p", tag="slot_w2p", align_bytes=64)
        rows_a = keep.tile([P, R + J], U8, name="rows_a", align_bytes=64)
        rows_b = keep.tile([P, R + J], U8, name="rows_b", tag="slot_rows", align_bytes=64)
        x1s = keep.tile([P, J], U8, name="x1s", align_bytes=64)
        x2s = keep.tile([P, J], U8, name="x2s", align_bytes=64)
        x1w = keep.tile([P, J], U16, name="x1w", tag="slot_x1w", align_bytes=64)
        x2w = keep.tile([P, J], U16, name="x2w", tag="slot_x2w", align_bytes=64)

        nc.vector.tensor_copy(x1s[:], xs[:].indirect(l1[:]))
        deal(rows_a[:, 0:R], wsr[:, 0:R])
        nc.vector.tensor_copy(rows_a[:, R : R + J].bitcast(U32), x1s[:].bitcast(U32))
        carry(nc.scalar, plane_a, rows_a)
        nc.vector.tensor_copy(x1w[:], xw[:].indirect(l1[:]))
        deal(wp[:], wr[:])
        nc.vector.tensor_copy(x2s[:], xs[:].indirect(l2[:]))
        deal(rows_b[:, 0:R], wsr[:, R : 2 * R])
        nc.vector.tensor_copy(rows_b[:, R : R + J].bitcast(U32), x2s[:].bitcast(U32))
        carry(nc.sync, plane_b, rows_b)
        deal(w2p[:], w2r[:])
        nc.vector.tensor_copy(x2w[:], xw[:].indirect(l2[:]))

        rows_late = keep.tile([P, 3 * N], U8, name="rows_late", tag="slot_rows", align_bytes=64)
        load_rows(rows_late[:, 0:N], ws_scales)
        load_rows(rows_late[:, N : 2 * N], sx_scales)
        load_rows(rows_late[:, 2 * N : 3 * N], wb_scales)
        carry(nc.sync, late, rows_late)

        def first_stage(bank, wq, fmt, xq, plane, t):
            nc.tensor.matmul_mx(
                out=bank, lhsT=wq[:, t * P : (t + 1) * P].bitcast(fmt), lhsT_scale=plane[:, t * P : (t + 1) * P],
                rhs=xq[:].bitcast(E2M1), rhs_scale=plane[:, R : R + J], start=True, stop=True,
            )

        pa = [psum.tile([P, BANK], F32, name="pa%d" % t, tag="bank%d" % t) for t in range(PACK)]
        pb = [psum.tile([P, 2, J], F32, name="pb%d" % e, tag="bank%d" % (PACK + e)) for e in range(2)]
        for t in SCALAR_SLICES + VECTOR_SLICES:
            first_stage(pa[t][:, 0:J], wp, E5M2, x1w, plane_a, t)
        for t in range(PACK):
            first_stage(pb[t // 2][:, t % 2, :], w2p, E4M3, x2w, plane_b, t)

        skip = keep.tile([P, N + O], U32, name="skip", tag="slot_x2w", align_bytes=64)
        wsw = skip[:, 0:N]
        sxw = skip[:, N : N + O]
        wbw = keep.tile([P, N], U32, name="wbw", tag="slot_x1w", align_bytes=64)
        nc.sync.dma_start(wsw[:].bitcast(I32), words_view(ws_words))
        nc.sync.dma_start(sxw[:].bitcast(I32), words_view(sx_words))
        nc.sync.dma_start(wbw[:].bitcast(I32), words_view(wb_words))

        pv = [
            reuse.tile([P, C], F32, name="pv0", offset=0),
            keep.tile([P, C], F32, name="pv1", tag="slot_w", align_bytes=64),
            reuse.tile([P, C], F32, name="pv2", offset=4 * C),
            keep.tile([P, C], F32, name="pv3", tag="slot_w2p", align_bytes=64),
        ]
        for t in range(PACK):
            nc.gpsimd.memset(pv[t][:], 0.0)
        a = [
            keep.tile([P, J], F32, name="a%d" % t, tag="slot_w2r" if t == VECTOR_SLICES[-1] else "a%d" % t, align_bytes=64)
            for t in range(PACK)
        ]
        b = [keep.tile([P, J], F32, name="b%d" % t) for t in range(PACK)]
        g = [keep.tile([P, O], F32, name="g%d" % t) for t in range(PACK)]
        d_lo = keep.tile([P, 2, O], F32, name="d_lo")
        d_hi = [keep.tile([P, 2, HALF], F32, name="d_hi%d" % h) for h in range(2)]

        def fetch(t, dst, bank):
            if t in SCALAR_SLICES:
                nc.scalar.activation(dst, bank, ACT.Copy)
            else:
                nc.vector.tensor_copy(dst, bank)

        def put(t, board, lst, src):
            if t in SCALAR_SLICES:
                nc.scalar.activation(board[t][:].indirect(lst[:]), src[t][:], ACT.Copy)
            else:
                nc.vector.tensor_copy(board[t][:].indirect(lst[:]), src[t][:])

        def look_v(dst, t, lo, hi):
            nc.vector.tensor_tensor(dst, pv[t][:].indirect(l6[:, lo // GROUP : hi // GROUP]), g[t][:, lo:hi], ALU.subtract)

        for t in SCALAR_SLICES + VECTOR_SLICES:
            fetch(t, a[t][:], pa[t][:, 0:J])
        for u in range(2):
            put(SCALAR_SLICES[u], pw, l3, a)
            put(VECTOR_SLICES[u], pw, l3, a)
        for t in range(PACK):
            fetch(t, b[t][:], pb[t // 2][:, t % 2, :])
        for u in range(2):
            put(VECTOR_SLICES[u], pv, l4, b)
            put(SCALAR_SLICES[u], pv, l4, b)

        py0 = psum.tile([P, BANK], F32, name="py0", tag="bank0")
        py1 = [psum.tile([P, BANK], F32, name="py1%d" % m, tag="bank%d" % (1 + m)) for m in range(2)]

        def sums(h, m):
            return py0[:, m * HALF : (m + 1) * HALF] if h == 0 else py1[m][:, 0:HALF]

        for h in range(2):
            for m in range(2):
                nc.tensor.matmul_mx(
                    out=sums(h, m), lhsT=wsw[:, m * P : (m + 1) * P].bitcast(E4M3),
                    lhsT_scale=late[:, m * P : (m + 1) * P],
                    rhs=sxw[:, h * HALF : (h + 1) * HALF].bitcast(E5M2), rhs_scale=late[:, N + h * HALF : N + (h + 1) * HALF],
                    start=(h == 1 or m == 0), stop=False,
                )

        hid = [keep.tile([P, HALF, PACK], BF16, name="hid%d" % h, align_bytes=64) for h in range(2)]
        hq = [keep.tile([P, HALF], U32, name="hq%d" % h, align_bytes=64) for h in range(2)]
        hs = [keep.tile([P, HALF], U8, name="hs%d" % h, align_bytes=64) for h in range(2)]
        y0 = keep.tile([P, 2, HALF], F32, name="y0")
        y1 = [keep.tile([P, HALF], F32, name="y1%d" % m) for m in range(2)]

        for t in range(PACK):
            nc.scalar.activation(g[t][:], pw[t][:].indirect(l5[:]), ACT.Copy)
        for u in range(2):
            look_v(d_lo[:, u, :], u, 0, O)
        for u in range(2):
            for h in range(2):
                look_v(d_hi[h][:, u, :], 2 + u, h * HALF, (h + 1) * HALF)
        for h in range(2):
            nc.scalar.activation(hid[h][:, :, 0:2], d_lo[:, :, h * HALF : (h + 1) * HALF].rearrange("p t o -> p o t"), ACT.Abs)
        for h in range(2):
            nc.scalar.activation(hid[h][:, :, 2:4], d_hi[h][:].rearrange("p t o -> p o t"), ACT.Abs)
            nc.vector.quantize_mx(out=hq[h][:].bitcast(E5M2), scales=hs[h][:], in_=hid[h][:].rearrange("p o t -> p (o t)"))
            for m in range(2):
                nc.tensor.matmul_mx(
                    out=sums(h, m), lhsT=wbw[:, m * P : (m + 1) * P].bitcast(E4M3),
                    lhsT_scale=late[:, 2 * N + m * P : 2 * N + (m + 1) * P],
                    rhs=hq[h][:].bitcast(E5M2), rhs_scale=hs[h][:],
                    start=False, stop=(h == 1 or m == 1),
                )
        nc.scalar.copy(y0[:].rearrange("p m o -> p (m o)"), py0[:, 0 : 2 * HALF])
        nc.sync.dma_start(out.rearrange("(m p) o -> p m o", p=P)[:, :, 0:HALF], y0[:])
        nc.scalar.copy(y1[0][:], sums(1, 0))
        nc.vector.tensor_copy(y1[1][:], sums(1, 1))
        nc.scalar.dma_start(out[0:P, HALF:O], y1[0][:])
        nc.sync.dma_start(out[P:N, HALF:O], y1[1][:])
